import numpy as np
import ml_dtypes


def mxq(x, axis, fmt="e4m3"):
    dtype, down = {"e4m3": (ml_dtypes.float8_e4m3fn, 7), "e5m2": (ml_dtypes.float8_e5m2, 14)}[fmt]
    v = np.moveaxis(np.asarray(x, np.float32).astype(ml_dtypes.bfloat16).astype(np.float64), axis, -1)
    blocks = v.reshape(v.shape[:-1] + (-1, 32))
    amax = np.abs(blocks).max(-1, keepdims=True)
    byte = np.maximum(np.where(amax > 0, np.frexp(amax)[1] - 1 + 127, 0) - down, 1)
    scale = np.exp2(byte - 127.0)
    codes = (blocks / scale).astype(np.float32).astype(dtype).astype(np.float64)
    return np.moveaxis((codes * scale).reshape(v.shape), -1, axis)


WIDE = False


def mx_kscale(k):
    if not WIDE:
        return np.ones(k)
    levels = np.array([30, -30])
    if k % 512:
        return np.exp2(np.random.permutation(np.resize(levels, k // 32))).repeat(32)
    a = np.empty((k // 512, 16))
    for p in range(k // 512):
        a[p, :8] = np.random.permutation(np.resize(levels, 8))
        for g in range(8):
            far = levels[np.abs(levels - a[p, g]) >= 10]
            a[p, g + 8] = far[np.random.randint(len(far))]
    return np.exp2(a.ravel()).repeat(32)


def f64(x):
    return np.asarray(x).astype(np.float64)


def striped(idx):
    return np.tile(np.asarray(idx).reshape(-1, 16).T, (8, 1)).astype(np.uint16)


def unstriped(offs):
    return offs[:16].T.reshape(-1).astype(np.int64)


E2M1 = np.array([0.0, 0.5, 1.0, 1.5, 2.0, 3.0, 4.0, 6.0, -0.0, -0.5, -1.0, -1.5, -2.0, -3.0, -4.0, -6.0])


def pack_weight(w, fmt):
    k, n = w.shape
    w = f64(np.asarray(w, np.float32).astype(ml_dtypes.bfloat16)).reshape(k // 32, 32, n)
    amax = np.abs(w).max(1)
    if fmt == "e4m3":
        byte = np.frexp(amax)[1] - 1 + 127 - 7
    else:
        mant, ex = np.frexp(amax / 6.0)
        byte = np.where(mant > 0.5, ex, ex - 1) + 127
    byte = np.clip(np.where(amax > 0, byte, 1), 1, 254)
    scaled = (w * np.exp2(127.0 - byte)[:, None, :]).reshape(k, n).astype(np.float32)
    by_word = np.ascontiguousarray(scaled.reshape(k // 512, 128, 4, n).transpose(0, 1, 3, 2))
    if fmt == "e4m3":
        words = by_word.astype(ml_dtypes.float8_e4m3fn).view(np.uint8)
    else:
        c = by_word.astype(ml_dtypes.float4_e2m1fn).view(np.uint8) & 0xF
        words = (c[..., 0::2] | (c[..., 1::2] << 4)).reshape(k // 512, 128, 2 * n)
    return np.ascontiguousarray(words), np.ascontiguousarray(byte.astype(np.uint8).reshape(k // 512, 16, n))


def unpack_weight(words, scales, fmt):
    g, _, n = scales.shape
    words = np.ascontiguousarray(words).reshape(g, 128, n, -1)
    if fmt == "e4m3":
        vals = words.view(ml_dtypes.float8_e4m3fn).astype(np.float64)
    else:
        nib = np.empty((g, 128, n, 4), np.uint8)
        nib[..., 0::2] = words & 0xF
        nib[..., 1::2] = words >> 4
        vals = E2M1[nib]
    vals = vals * np.repeat(np.exp2(scales.astype(np.float64) - 127.0), 8, axis=1)[..., None]
    return vals.transpose(0, 1, 3, 2).reshape(g * 512, n)


def sigmoid(v):
    return 1.0 / (1.0 + np.exp(-v))


def sgn(shape):
    return np.random.uniform(0.5, 2.0, shape) * np.where(np.random.standard_normal(shape) < 0, -1.0, 1.0)


K, T, J, R, F, Z, C, O, N = 512, 1024, 256, 512, 512, 1024, 512, 256, 256


def setup_inputs():
    n = np.random.standard_normal
    idx = np.random.permutation(T)[:J]
    idx2 = np.random.permutation(Z)[:J]
    idx3 = np.random.permutation(C)[:J]
    idx4 = np.random.permutation(C)[:C]
    idx5 = np.random.permutation(C)[:C]
    idx6 = np.random.permutation(C)[:O]
    idx7 = np.random.permutation(T)[:O]
    fk = mx_kscale(K)
    ff = mx_kscale(F)
    fr = mx_kscale(R)
    xtp = pack_weight(n((K, T)) / fk[:, None], "e2m1")
    xop = pack_weight(n((F, Z)) / ff[:, None], "e4m3")
    wp = pack_weight(n((K, R)) * 1 / np.sqrt(K) * fk[:, None], "e4m3")
    w0p = pack_weight(n((F, R)) * 1 / np.sqrt(F) * ff[:, None], "e2m1")
    wbp = pack_weight(n((R, N)) * 1 / np.sqrt(R) / fr[:, None], "e2m1")
    wsp = pack_weight(n((K, N)) * 1 / np.sqrt(K) * fk[:, None], "e4m3")
    return {
        "xt_words": xtp[0],
        "xt_scales": xtp[1],
        "xo_words": xop[0],
        "xo_scales": xop[1],
        "w_words": wp[0],
        "w_scales": wp[1],
        "w0_words": w0p[0],
        "w0_scales": w0p[1],
        "sa": (sgn((R, 1))).astype(np.float32),
        "sb": (np.random.uniform(0.5, 1.6, (R, 1)) * fr[:, None]).astype(np.float32),
        "sg": (sgn((R, 1))).astype(np.float32),
        "bg": (np.random.uniform(-2.0, 2.0, (R, 1))).astype(np.float32),
        "wb_words": wbp[0],
        "wb_scales": wbp[1],
        "ws_words": wsp[0],
        "ws_scales": wsp[1],
        "offs": striped(idx),
        "offs2": striped(idx2),
        "offs3": striped(idx3),
        "offs4": striped(idx4),
        "offs5": striped(idx5),
        "offs6": striped(idx6),
        "offs7": striped(idx7),
    }


def reference(xt_words, xt_scales, xo_words, xo_scales, w_words, w_scales, w0_words, w0_scales, sa, sb, sg, bg, wb_words, wb_scales, ws_words, ws_scales, offs, offs2, offs3, offs4, offs5, offs6, offs7):
    idx = unstriped(offs)
    idx2 = unstriped(offs2)
    idx3 = unstriped(offs3)
    idx4 = unstriped(offs4)
    idx5 = unstriped(offs5)
    idx6 = unstriped(offs6)
    idx7 = unstriped(offs7)
    xtu = unpack_weight(xt_words, xt_scales, "e2m1")
    xou = unpack_weight(xo_words, xo_scales, "e4m3")
    wu = unpack_weight(w_words, w_scales, "e4m3")
    w0u = unpack_weight(w0_words, w0_scales, "e2m1")
    wbu = unpack_weight(wb_words, wb_scales, "e2m1")
    wsu = unpack_weight(ws_words, ws_scales, "e4m3")
    xtidxg = xtu[:, idx]
    xoidx2g = xou[:, idx2]
    a = wu.T @ xtidxg + w0u.T @ xoidx2g
    pw = np.zeros((R, C))
    pw[:, idx3] = a
    pg = np.maximum(pw, pw[:, idx4] * f64(sa) * sigmoid(pw[:, idx5] * f64(sg) + f64(bg)))
    hid = pg[:, idx6] * f64(sb)
    hidq = mxq(hid, 0, "e5m2")
    xtidx7g = xtu[:, idx7]
    y = wbu.T @ hidq + wsu.T @ xtidx7g
    return y

@@ -1,0 +1,195 @@
+from contextlib import ExitStack
+
+import concourse.mybir as mybir
+
+K, T, J, R, F, Z, C, O, N = 512, 1024, 256, 512, 512, 1024, 512, 256, 256
+FLOPS = 2 * (K * R * J + F * R * J + R * N * O + K * N * O)
+
+F32 = mybir.dt.float32
+BF16 = mybir.dt.bfloat16
+I32 = mybir.dt.int32
+U32 = mybir.dt.uint32
+U16 = mybir.dt.uint16
+U8 = mybir.dt.uint8
+E4M3 = mybir.dt.float8_e4m3fn_x4
+E5M2 = mybir.dt.float8_e5m2_x4
+E2M1 = mybir.dt.float4_e2m1fn_x4
+ACT = mybir.ActivationFunctionType
+ALU = mybir.AluOpType
+
+P = 128
+PACK = 4
+QUADS = 4
+BOARD = 2 * C
+HALF = O // 2
+
+
+def tile_list_gatedladder_bank_further_plain_kernel(
+    tc, xt_words, xt_scales, xo_words, xo_scales, w_words, w_scales, w0_words, w0_scales,
+    sa, sb, sg, bg, wb_words, wb_scales, ws_words, ws_scales,
+    offs, offs2, offs3, offs4, offs5, offs6, offs7, out,
+):
+    nc = tc.nc
+    with ExitStack() as ctx:
+        keep = ctx.enter_context(tc.tile_pool(name="keep", bufs=1))
+        psum = ctx.enter_context(tc.psum_pool(name="psum", bufs=1))
+
+        def sb_tile(name, shape, dtype):
+            return keep.tile(shape, dtype, name=name, align_bytes=64)
+
+        def load_list(name, src):
+            lst = keep.tile(list(src.shape), U16, name=name)
+            nc.sync.dma_start(lst[:], src)
+            return lst
+
+        def load_words(queue, tile, src):
+            queue.dma_start(tile[:].bitcast(I32), src.bitcast(I32))
+
+        def load_plane(queue, plane, src):
+            rows = src[0].bitcast(I32)
+            for q in range(QUADS):
+                queue.dma_start(plane.bitcast(I32)[32 * q : 32 * q + 4, :], rows[4 * q : 4 * q + 4, :])
+
+        def load_rows(queue, name, src):
+            vec = keep.tile([P, PACK], F32, name=name)
+            queue.dma_start(vec[:], src.rearrange("(p t) o -> p (t o)", t=PACK))
+            return vec
+
+        xt_w = sb_tile("xt_w", [P, T], U16)
+        xt_s = sb_tile("xt_s", [P, T], U8)
+        xo_w = sb_tile("xo_w", [P, Z], U32)
+        xo_s = sb_tile("xo_s", [P, Z], U8)
+        w_raw = sb_tile("w_raw", [P, R], U32)
+        w0_raw = sb_tile("w0_raw", [P, R], U16)
+        first_s_stage = sb_tile("first_s_stage", [4, QUADS, 2 * R // 4], I32)
+        first_s_raw = sb_tile("first_s_raw", [P, 2 * R], U8)
+        last_s = sb_tile("last_s", [P, 2 * N], U8)
+        boards = [sb_tile("board%d" % t, [P, BOARD], F32) for t in range(PACK)]
+
+        nc.vector.memset(xt_s[:].bitcast(I32), 0)
+        nc.vector.memset(xo_s[:].bitcast(I32), 0)
+        nc.vector.memset(first_s_raw[:].bitcast(I32), 0)
+        for s, src in enumerate((w_scales, w0_scales)):
+            nc.gpsimd.dma_start(
+                first_s_stage[:, :, s * (R // 4) : (s + 1) * (R // 4)],
+                src[0].bitcast(I32).rearrange("(q r) c -> r q c", r=4),
+            )
+        for t in range(PACK):
+            eng = nc.vector if t < 2 else nc.gpsimd
+            eng.memset(boards[t][:, 0:C], 0.0)
+        nc.gpsimd.memset(last_s[:].bitcast(I32), 0)
+
+        load_words(nc.sync, xt_w, xt_words[0])
+        idx = load_list("idx", offs)
+        load_plane(nc.scalar, xt_s[:], xt_scales)
+        load_words(nc.sync, xo_w, xo_words[0].rearrange("p c t -> p (c t)"))
+        idx2 = load_list("idx2", offs2)
+        load_words(nc.sync, w_raw, w_words[0].rearrange("p c t -> p (c t)"))
+        load_words(nc.sync, w0_raw, w0_words[0])
+        load_plane(nc.scalar, xo_s[:], xo_scales)
+        idx7 = load_list("idx7", offs7)
+        idx3 = load_list("idx3", offs3)
+        idx5 = load_list("idx5", offs5)
+        slope = load_rows(nc.sync, "slope", sg)
+        offset = load_rows(nc.sync, "offset", bg)
+        idx4 = load_list("idx4", offs4)
+        first_weight = load_rows(nc.sync, "first_weight", sa)
+        idx6 = load_list("idx6", offs6)
+        second_weight = load_rows(nc.sync, "second_weight", sb)
+        ws_w = sb_tile("ws_w", [P, N], U32)
+        wb_w = sb_tile("wb_w", [P, N], U16)
+        load_words(nc.sync, ws_w, ws_words[0].rearrange("p c t -> p (c t)"))
+        load_plane(nc.sync, last_s[:, 0:N], ws_scales)
+        load_words(nc.sync, wb_w, wb_words[0])
+        load_plane(nc.sync, last_s[:, N : 2 * N], wb_scales)
+
+        def gather(name, table, lst, dtype):
+            picked = sb_tile(name, [P, 16 * lst.shape[1]], dtype)
+            nc.vector.tensor_copy(picked[:], table[:].indirect(lst[:]))
+            return picked
+
+        tok_w = gather("tok_w", xt_w, idx, U16)
+        tok_s = gather("tok_s", xt_s, idx, U8)
+        note_w = gather("note_w", xo_w, idx2, U32)
+        for q in range(QUADS):
+            nc.vector.tensor_copy(first_s_raw[:].bitcast(I32)[32 * q : 32 * q + 4, :], first_s_stage[:, q, :])
+        note_s = gather("note_s", xo_s, idx2, U8)
+
+        w_dealt = sb_tile("w_dealt", [P, PACK, P], U32)
+        w0_dealt = sb_tile("w0_dealt", [P, PACK, P], U16)
+        nc.scalar.copy(w_dealt[:].rearrange("p t m -> p m t"), w_raw[:].rearrange("p (m t) -> p m t", t=PACK))
+        nc.scalar.copy(w0_dealt[:], w0_raw[:].rearrange("p (m t) -> p t m", t=PACK))
+        first_s = []
+        for pair in range(2):
+            dealt = sb_tile("first_s%d" % pair, [P, 2, 2, P], U8)
+            nc.vector.tensor_copy(
+                dealt[:],
+                first_s_raw[:].rearrange("p (s m t) -> p s t m", s=2, t=PACK)[:, :, 2 * pair : 2 * pair + 2, :],
+            )
+            first_s.append(dealt)
+
+        hidden = []
+        for t in range(PACK):
+            acc = psum.tile([P, J], F32, name="hidden_acc%d" % t)
+            scales = first_s[t // 2]
+            nc.tensor.matmul_mx(acc[:], lhsT=w_dealt[:, t, :].bitcast(E4M3), lhsT_scale=scales[:, 0, t % 2, :],
+                                rhs=tok_w[:].bitcast(E2M1), rhs_scale=tok_s[:], start=True, stop=False)
+            nc.tensor.matmul_mx(acc[:], lhsT=w0_dealt[:, t, :].bitcast(E2M1), lhsT_scale=scales[:, 1, t % 2, :],
+                                rhs=note_w[:].bitcast(E4M3), rhs_scale=note_s[:], start=False, stop=True)
+            a_t = sb_tile("hidden%d" % t, [P, J], F32)
+            nc.scalar.copy(a_t[:], acc[:])
+            hidden.append(a_t)
+
+        short_w = gather("short_w", xt_w, idx7, U16)
+        short_s = gather("short_s", xt_s, idx7, U8)
+
+        for t in range(PACK):
+            nc.vector.tensor_copy(boards[t][:].indirect(idx3[:]), hidden[t][:])
+
+        result_acc = {}
+        for h in range(2):
+            for b in range(N // P):
+                acc = psum.tile([P, HALF], F32, name="result_acc%d%d" % (h, b))
+                nc.tensor.matmul_mx(acc[:], lhsT=ws_w[:, b * P : (b + 1) * P].bitcast(E4M3),
+                                    lhsT_scale=last_s[:, b * P : (b + 1) * P],
+                                    rhs=short_w[:, h * HALF : (h + 1) * HALF].bitcast(E2M1),
+                                    rhs_scale=short_s[:, h * HALF : (h + 1) * HALF], start=True, stop=False)
+                result_acc[(h, b)] = acc
+
+        kept = []
+        for t in range(PACK):
+            gate = sb_tile("gate%d" % t, [P, C], F32)
+            weighted = sb_tile("weighted%d" % t, [P, C], F32)
+            nc.scalar.activation(gate[:], boards[t][:].indirect(idx5[:]), ACT.Sigmoid,
+                                 bias=offset[:, t : t + 1], scale=slope[:, t : t + 1])
+            nc.scalar.activation(weighted[:], boards[t][:].indirect(idx4[:]), ACT.Copy, scale=first_weight[:, t : t + 1])
+            gated = sb_tile("gated%d" % t, [P, C], F32)
+            nc.vector.tensor_tensor(gated[:], weighted[:], gate[:], ALU.mult)
+            kept_t = sb_tile("kept%d" % t, [P, C], F32)
+            nc.vector.tensor_tensor(kept_t[:], boards[t][:, 0:C], gated[:], ALU.max)
+            kept.append(kept_t)
+
+        out_view = out.rearrange("(b p) o -> p b o", p=P)
+        for h in range(2):
+            hid = sb_tile("hid%d" % h, [P, PACK, HALF], F32)
+            cols = HALF // 16
+            for t in range(PACK):
+                nc.scalar.activation(hid[:, t, :], kept[t][:].indirect(idx6[:, h * cols : (h + 1) * cols]), ACT.Copy,
+                                     scale=second_weight[:, t : t + 1])
+            woven = sb_tile("woven%d" % h, [P, HALF, PACK], BF16)
+            nc.vector.tensor_copy(woven[:].rearrange("p (c i) t -> p c t i", i=4),
+                                  hid[:].rearrange("p t (c i) -> p c t i", i=4))
+            hid_w = sb_tile("hid_w%d" % h, [P, HALF], U32)
+            hid_s = sb_tile("hid_s%d" % h, [P, HALF], U8)
+            nc.vector.quantize_mx(hid_w[:].bitcast(E5M2), hid_s[:], woven[:].rearrange("p c t -> p (c t)"))
+            result = sb_tile("result%d" % h, [P, N // P, HALF], F32)
+            for b in range(N // P):
+                acc = result_acc[(h, b)]
+                nc.tensor.matmul_mx(acc[:], lhsT=wb_w[:, b * P : (b + 1) * P].bitcast(E2M1),
+                                    lhsT_scale=last_s[:, N + b * P : N + (b + 1) * P],
+                                    rhs=hid_w[:].bitcast(E5M2), rhs_scale=hid_s[:], start=False, stop=True)
+                if b == 0:
+                    nc.vector.tensor_copy(result[:, b, :], acc[:])
+                else:
+                    nc.scalar.copy(result[:, b, :], acc[:])
+            nc.sync.dma_start(out_view[:, :, h * HALF : (h + 1) * HALF], result[:])

@@ -45,10 +45,10 @@ def tile_list_gatedladder_bank_further_plain_kernel(
         def load_words(queue, tile, src):
             queue.dma_start(tile[:].bitcast(I32), src.bitcast(I32))
 
-        def load_plane(queue, plane, src):
+        def load_plane(queues, plane, src):
             rows = src[0].bitcast(I32)
             for q in range(QUADS):
-                queue.dma_start(plane.bitcast(I32)[32 * q : 32 * q + 4, :], rows[4 * q : 4 * q + 4, :])
+                queues[q].dma_start(plane.bitcast(I32)[32 * q : 32 * q + 4, :], rows[4 * q : 4 * q + 4, :])
 
         def load_rows(queue, name, src):
             vec = keep.tile([P, PACK], F32, name=name)
@@ -66,85 +66,115 @@ def tile_list_gatedladder_bank_further_plain_kernel(
         last_s = sb_tile("last_s", [P, 2 * N], U8)
         boards = [sb_tile("board%d" % t, [P, BOARD], F32) for t in range(PACK)]
 
-        nc.vector.memset(xt_s[:].bitcast(I32), 0)
-        nc.vector.memset(xo_s[:].bitcast(I32), 0)
-        nc.vector.memset(first_s_raw[:].bitcast(I32), 0)
-        for s, src in enumerate((w_scales, w0_scales)):
-            nc.gpsimd.dma_start(
+        def stage_scales(queue, s, src):
+            queue.dma_start(
                 first_s_stage[:, :, s * (R // 4) : (s + 1) * (R // 4)],
                 src[0].bitcast(I32).rearrange("(q r) c -> r q c", r=4),
             )
-        for t in range(PACK):
-            eng = nc.vector if t < 2 else nc.gpsimd
-            eng.memset(boards[t][:, 0:C], 0.0)
-        nc.gpsimd.memset(last_s[:].bitcast(I32), 0)
 
-        load_words(nc.sync, xt_w, xt_words[0])
+        nc.vector.memset(xt_s[:].bitcast(I32), 0)
+        nc.vector.memset(xo_s[:].bitcast(I32), 0)
+        nc.vector.memset(first_s_raw[:].bitcast(I32), 0)
+        nc.vector.memset(boards[0][:, 0:C], 0.0)
+
+        stage_scales(nc.gpsimd, 1, w0_scales)
+        for t in range(1, PACK):
+            nc.gpsimd.memset(boards[t][:, 0:C], 0.0)
+        nc.gpsimd.memset(last_s[:].bitcast(I32), 0)
+        slope = load_rows(nc.gpsimd, "slope", sg)
+        offset = load_rows(nc.gpsimd, "offset", bg)
+        second_weight = load_rows(nc.gpsimd, "second_weight", sb)
+
         idx = load_list("idx", offs)
-        load_plane(nc.scalar, xt_s[:], xt_scales)
-        load_words(nc.sync, xo_w, xo_words[0].rearrange("p c t -> p (c t)"))
+        load_words(nc.scalar, xt_w, xt_words[0])
+        load_plane([nc.scalar, nc.sync, nc.scalar, nc.sync], xt_s[:], xt_scales)
+        stage_scales(nc.sync, 0, w_scales)
+        load_words(nc.scalar, xo_w, xo_words[0].rearrange("p c t -> p (c t)"))
+        load_plane([nc.sync] * QUADS, xo_s[:], xo_scales)
+        load_words(nc.scalar, w_raw, w_words[0].rearrange("p c t -> p (c t)"))
+        load_words(nc.scalar, w0_raw, w0_words[0])
+        warm_in = sb_tile("warm_in", [P, 1], F32)
+        warm_out = sb_tile("warm_out", [P, 1], F32)
+        nc.vector.memset(warm_in[:], 0.0)
+        nc.scalar.activation(warm_out[:], warm_in[:], ACT.Sigmoid)
         idx2 = load_list("idx2", offs2)
-        load_words(nc.sync, w_raw, w_words[0].rearrange("p c t -> p (c t)"))
-        load_words(nc.sync, w0_raw, w0_words[0])
-        load_plane(nc.scalar, xo_s[:], xo_scales)
-        idx7 = load_list("idx7", offs7)
         idx3 = load_list("idx3", offs3)
         idx5 = load_list("idx5", offs5)
-        slope = load_rows(nc.sync, "slope", sg)
-        offset = load_rows(nc.sync, "offset", bg)
         idx4 = load_list("idx4", offs4)
         first_weight = load_rows(nc.sync, "first_weight", sa)
+        idx7 = load_list("idx7", offs7)
         idx6 = load_list("idx6", offs6)
-        second_weight = load_rows(nc.sync, "second_weight", sb)
         ws_w = sb_tile("ws_w", [P, N], U32)
         wb_w = sb_tile("wb_w", [P, N], U16)
         load_words(nc.sync, ws_w, ws_words[0].rearrange("p c t -> p (c t)"))
-        load_plane(nc.sync, last_s[:, 0:N], ws_scales)
+        load_plane([nc.sync] * QUADS, last_s[:, 0:N], ws_scales)
         load_words(nc.sync, wb_w, wb_words[0])
-        load_plane(nc.sync, last_s[:, N : 2 * N], wb_scales)
+        load_plane([nc.sync] * QUADS, last_s[:, N : 2 * N], wb_scales)
 
         def gather(name, table, lst, dtype):
             picked = sb_tile(name, [P, 16 * lst.shape[1]], dtype)
-            nc.vector.tensor_copy(picked[:], table[:].indirect(lst[:]))
+            nc.vector.tensor_copy(picked[:], table[:].indirect(lst))
             return picked
 
-        tok_w = gather("tok_w", xt_w, idx, U16)
-        tok_s = gather("tok_s", xt_s, idx, U8)
-        note_w = gather("note_w", xo_w, idx2, U32)
+        tok_w = gather("tok_w", xt_w, idx[:], U16)
+        tok_s = gather("tok_s", xt_s, idx[:], U8)
         for q in range(QUADS):
             nc.vector.tensor_copy(first_s_raw[:].bitcast(I32)[32 * q : 32 * q + 4, :], first_s_stage[:, q, :])
-        note_s = gather("note_s", xo_s, idx2, U8)
+        by_slot = first_s_raw[:].rearrange("p (s m t) -> p s t m", s=2, t=PACK)
+        first_s_head = sb_tile("first_s_head", [P, 2, 1, P], U8)
+        nc.vector.tensor_copy(first_s_head[:], by_slot[:, :, 0:1, :])
 
-        w_dealt = sb_tile("w_dealt", [P, PACK, P], U32)
-        w0_dealt = sb_tile("w0_dealt", [P, PACK, P], U16)
-        nc.scalar.copy(w_dealt[:].rearrange("p t m -> p m t"), w_raw[:].rearrange("p (m t) -> p m t", t=PACK))
-        nc.scalar.copy(w0_dealt[:], w0_raw[:].rearrange("p (m t) -> p t m", t=PACK))
-        first_s = []
-        for pair in range(2):
-            dealt = sb_tile("first_s%d" % pair, [P, 2, 2, P], U8)
-            nc.vector.tensor_copy(
-                dealt[:],
-                first_s_raw[:].rearrange("p (s m t) -> p s t m", s=2, t=PACK)[:, :, 2 * pair : 2 * pair + 2, :],
-            )
-            first_s.append(dealt)
+        note_w = sb_tile("note_w", [P, J], U32)
+        note_s = sb_tile("note_s", [P, J], U8)
+        for h in range(2):
+            part = idx2[:, h * (P // 16) : (h + 1) * (P // 16)]
+            nc.vector.tensor_copy(note_w[:, h * P : (h + 1) * P], xo_w[:].indirect(part))
+            nc.vector.tensor_copy(note_s[:, h * P : (h + 1) * P], xo_s[:].indirect(part))
 
-        hidden = []
-        for t in range(PACK):
-            acc = psum.tile([P, J], F32, name="hidden_acc%d" % t)
-            scales = first_s[t // 2]
-            nc.tensor.matmul_mx(acc[:], lhsT=w_dealt[:, t, :].bitcast(E4M3), lhsT_scale=scales[:, 0, t % 2, :],
-                                rhs=tok_w[:].bitcast(E2M1), rhs_scale=tok_s[:], start=True, stop=False)
-            nc.tensor.matmul_mx(acc[:], lhsT=w0_dealt[:, t, :].bitcast(E2M1), lhsT_scale=scales[:, 1, t % 2, :],
-                                rhs=note_w[:].bitcast(E4M3), rhs_scale=note_s[:], start=False, stop=True)
-            a_t = sb_tile("hidden%d" % t, [P, J], F32)
-            nc.scalar.copy(a_t[:], acc[:])
-            hidden.append(a_t)
+        w_head = sb_tile("w_head", [P, 1, P], U32)
+        w0_head = sb_tile("w0_head", [P, 1, P], U16)
+        w_rest = sb_tile("w_rest", [P, PACK - 1, P], U32)
+        w_by_slot = w_raw[:].rearrange("p (m t) -> p t m", t=PACK)
+        w0_by_slot = w0_raw[:].rearrange("p (m t) -> p t m", t=PACK)
+        nc.scalar.copy(w_head[:], w_by_slot[:, 0:1, :])
+        nc.scalar.copy(w0_head[:], w0_by_slot[:, 0:1, :])
+        nc.scalar.copy(w_rest[:].rearrange("p t m -> p m t"), w_raw[:].rearrange("p (m t) -> p m t", t=PACK)[:, :, 1:PACK])
+        first_s_rest = keep.tile([P, 2, PACK - 1, P], U8, name="first_s_rest", tag="xo_w", align_bytes=64)
+        nc.vector.tensor_copy(first_s_rest[:], by_slot[:, :, 1:PACK, :])
+        w0_rest = keep.tile([P, PACK - 1, P], U16, name="w0_rest", tag="xo_s", align_bytes=64)
+        nc.vector.tensor_copy(w0_rest[:], w0_by_slot[:, 1:PACK, :])
 
-        short_w = gather("short_w", xt_w, idx7, U16)
-        short_s = gather("short_s", xt_s, idx7, U8)
+        def first_stage(acc, w_cols, w0_cols, scales, u, cols):
+            nc.tensor.matmul_mx(acc, lhsT=w_cols[:, u, :].bitcast(E4M3), lhsT_scale=scales[:, 0, u, :],
+                                rhs=tok_w[:, cols].bitcast(E2M1), rhs_scale=tok_s[:, cols], start=True, stop=False)
+            nc.tensor.matmul_mx(acc, lhsT=w0_cols[:, u, :].bitcast(E2M1), lhsT_scale=scales[:, 1, u, :],
+                                rhs=note_w[:, cols].bitcast(E4M3), rhs_scale=note_s[:, cols], start=False, stop=True)
 
-        for t in range(PACK):
-            nc.vector.tensor_copy(boards[t][:].indirect(idx3[:]), hidden[t][:])
+        for h in range(2):
+            acc = psum.tile([P, P], F32, name="head_acc%d" % h)
+            first_stage(acc[:], w_head, w0_head, first_s_head, 0, slice(h * P, (h + 1) * P))
+            head = sb_tile("head%d" % h, [P, P], F32)
+            if h == 0:
+                nc.scalar.copy(head[:], acc[:])
+            else:
+                nc.vector.tensor_copy(head[:], acc[:])
+            nc.scalar.activation(boards[0][:].indirect(idx3[:, h * (P // 16) : (h + 1) * (P // 16)]), head[:], ACT.Copy)
+
+        acc1 = psum.tile([P, J], F32, name="acc1")
+        first_stage(acc1[:], w_rest, w0_rest, first_s_rest, 0, slice(0, J))
+        hidden1 = sb_tile("hidden1", [P, J], F32)
+        nc.vector.tensor_copy(hidden1[:], acc1[:])
+        nc.vector.tensor_copy(boards[1][:].indirect(idx3[:]), hidden1[:])
+        acc23 = psum.tile([P, 2, J], F32, name="acc23")
+        for u in range(2):
+            first_stage(acc23[:, u, :], w_rest, w0_rest, first_s_rest, 1 + u, slice(0, J))
+        hidden23 = sb_tile("hidden23", [P, 2, J], F32)
+        nc.vector.tensor_copy(hidden23[:], acc23[:])
+        for u in range(2):
+            nc.vector.tensor_copy(boards[2 + u][:].indirect(idx3[:]), hidden23[:, u, :])
+
+        short_w = gather("short_w", xt_w, idx7[:], U16)
+        short_s = gather("short_s", xt_s, idx7[:], U8)
 
         result_acc = {}
         for h in range(2):
@@ -188,8 +218,12 @@ def tile_list_gatedladder_bank_further_plain_kernel(
                 nc.tensor.matmul_mx(acc[:], lhsT=wb_w[:, b * P : (b + 1) * P].bitcast(E2M1),
                                     lhsT_scale=last_s[:, N + b * P : N + (b + 1) * P],
                                     rhs=hid_w[:].bitcast(E5M2), rhs_scale=hid_s[:], start=False, stop=True)
-                if b == 0:
+                if (h, b) == (1, 0):
                     nc.vector.tensor_copy(result[:, b, :], acc[:])
                 else:
                     nc.scalar.copy(result[:, b, :], acc[:])
-            nc.sync.dma_start(out_view[:, :, h * HALF : (h + 1) * HALF], result[:])
+            if h == 0:
+                nc.sync.dma_start(out_view[:, :, 0:HALF], result[:])
+            else:
+                nc.sync.dma_start(out_view[:, 0, HALF:O], result[:, 0, :])
+                nc.scalar.dma_start(out_view[:, 1, HALF:O], result[:, 1, :])

@@ -98,18 +98,18 @@ def tile_list_gatedladder_bank_further_plain_kernel(
         nc.vector.memset(warm_in[:], 0.0)
         nc.scalar.activation(warm_out[:], warm_in[:], ACT.Sigmoid)
         idx2 = load_list("idx2", offs2)
+        first_weight = load_rows(nc.scalar, "first_weight", sa)
         idx3 = load_list("idx3", offs3)
+        idx7 = load_list("idx7", offs7)
         idx5 = load_list("idx5", offs5)
         idx4 = load_list("idx4", offs4)
-        first_weight = load_rows(nc.sync, "first_weight", sa)
-        idx7 = load_list("idx7", offs7)
-        idx6 = load_list("idx6", offs6)
         ws_w = sb_tile("ws_w", [P, N], U32)
         wb_w = sb_tile("wb_w", [P, N], U16)
         load_words(nc.sync, ws_w, ws_words[0].rearrange("p c t -> p (c t)"))
         load_plane([nc.sync] * QUADS, last_s[:, 0:N], ws_scales)
         load_words(nc.sync, wb_w, wb_words[0])
         load_plane([nc.sync] * QUADS, last_s[:, N : 2 * N], wb_scales)
+        idx6 = load_list("idx6", offs6)
 
         def gather(name, table, lst, dtype):
             picked = sb_tile(name, [P, 16 * lst.shape[1]], dtype)
@@ -173,8 +173,10 @@ def tile_list_gatedladder_bank_further_plain_kernel(
         for u in range(2):
             nc.vector.tensor_copy(boards[2 + u][:].indirect(idx3[:]), hidden23[:, u, :])
 
-        short_w = gather("short_w", xt_w, idx7[:], U16)
-        short_s = gather("short_s", xt_s, idx7[:], U8)
+        short_w = keep.tile([P, O], U16, name="short_w", tag="w_head", align_bytes=64)
+        nc.vector.tensor_copy(short_w[:], xt_w[:].indirect(idx7[:]))
+        short_s = keep.tile([P, O], U8, name="short_s", tag="first_s_head", align_bytes=64)
+        nc.vector.tensor_copy(short_s[:], xt_s[:].indirect(idx7[:]))
 
         result_acc = {}
         for h in range(2):
@@ -190,13 +192,18 @@ def tile_list_gatedladder_bank_further_plain_kernel(
         for t in range(PACK):
             gate = sb_tile("gate%d" % t, [P, C], F32)
             weighted = sb_tile("weighted%d" % t, [P, C], F32)
-            nc.scalar.activation(gate[:], boards[t][:].indirect(idx5[:]), ACT.Sigmoid,
-                                 bias=offset[:, t : t + 1], scale=slope[:, t : t + 1])
-            nc.scalar.activation(weighted[:], boards[t][:].indirect(idx4[:]), ACT.Copy, scale=first_weight[:, t : t + 1])
             gated = sb_tile("gated%d" % t, [P, C], F32)
-            nc.vector.tensor_tensor(gated[:], weighted[:], gate[:], ALU.mult)
             kept_t = sb_tile("kept%d" % t, [P, C], F32)
-            nc.vector.tensor_tensor(kept_t[:], boards[t][:, 0:C], gated[:], ALU.max)
+            parts = 2 if t == PACK - 1 else 1
+            for part in range(parts):
+                cols = slice(part * C // parts, (part + 1) * C // parts)
+                entries = slice(cols.start // 16, cols.stop // 16)
+                nc.scalar.activation(gate[:, cols], boards[t][:].indirect(idx5[:, entries]), ACT.Sigmoid,
+                                     bias=offset[:, t : t + 1], scale=slope[:, t : t + 1])
+                nc.scalar.activation(weighted[:, cols], boards[t][:].indirect(idx4[:, entries]), ACT.Copy,
+                                     scale=first_weight[:, t : t + 1])
+                nc.vector.tensor_tensor(gated[:, cols], weighted[:, cols], gate[:, cols], ALU.mult)
+                nc.vector.tensor_tensor(kept_t[:, cols], boards[t][:, cols], gated[:, cols], ALU.max)
             kept.append(kept_t)
 
         out_view = out.rearrange("(b p) o -> p b o", p=P)

from contextlib import ExitStack

import concourse.mybir as mybir

K, T, J, R, F, Z, C, O, N = 512, 1024, 256, 512, 512, 1024, 512, 256, 256
FLOPS = 2 * (K * R * J + F * R * J + R * N * O + K * N * O)

F32 = mybir.dt.float32
BF16 = mybir.dt.bfloat16
I32 = mybir.dt.int32
U32 = mybir.dt.uint32
U16 = mybir.dt.uint16
U8 = mybir.dt.uint8
E4M3 = mybir.dt.float8_e4m3fn_x4
E5M2 = mybir.dt.float8_e5m2_x4
E2M1 = mybir.dt.float4_e2m1fn_x4
ACT = mybir.ActivationFunctionType
ALU = mybir.AluOpType

P = 128
PACK = 4
QUADS = 4
BOARD = 2 * C
HALF = O // 2


def tile_list_gatedladder_bank_further_plain_kernel(
    tc, xt_words, xt_scales, xo_words, xo_scales, w_words, w_scales, w0_words, w0_scales,
    sa, sb, sg, bg, wb_words, wb_scales, ws_words, ws_scales,
    offs, offs2, offs3, offs4, offs5, offs6, offs7, out,
):
    nc = tc.nc
    with ExitStack() as ctx:
        keep = ctx.enter_context(tc.tile_pool(name="keep", bufs=1))
        psum = ctx.enter_context(tc.psum_pool(name="psum", bufs=1))

        def sb_tile(name, shape, dtype):
            return keep.tile(shape, dtype, name=name, align_bytes=64)

        def load_list(name, src):
            lst = keep.tile(list(src.shape), U16, name=name)
            nc.sync.dma_start(lst[:], src)
            return lst

        def load_words(queue, tile, src):
            queue.dma_start(tile[:].bitcast(I32), src.bitcast(I32))

        def load_plane(queues, plane, src):
            rows = src[0].bitcast(I32)
            for q in range(QUADS):
                queues[q].dma_start(plane.bitcast(I32)[32 * q : 32 * q + 4, :], rows[4 * q : 4 * q + 4, :])

        def load_rows(queue, name, src):
            vec = keep.tile([P, PACK], F32, name=name)
            queue.dma_start(vec[:], src.rearrange("(p t) o -> p (t o)", t=PACK))
            return vec

        xt_w = sb_tile("xt_w", [P, T], U16)
        xt_s = sb_tile("xt_s", [P, T], U8)
        xo_w = sb_tile("xo_w", [P, Z], U32)
        xo_s = sb_tile("xo_s", [P, Z], U8)
        w_raw = sb_tile("w_raw", [P, R], U32)
        w0_raw = sb_tile("w0_raw", [P, R], U16)
        first_s_stage = sb_tile("first_s_stage", [4, QUADS, 2 * R // 4], I32)
        first_s_raw = sb_tile("first_s_raw", [P, 2 * R], U8)
        last_s = sb_tile("last_s", [P, 2 * N], U8)
        boards = [sb_tile("board%d" % t, [P, BOARD], F32) for t in range(PACK)]

        def stage_scales(queue, s, src):
            queue.dma_start(
                first_s_stage[:, :, s * (R // 4) : (s + 1) * (R // 4)],
                src[0].bitcast(I32).rearrange("(q r) c -> r q c", r=4),
            )

        nc.vector.memset(xt_s[:].bitcast(I32), 0)
        nc.vector.memset(xo_s[:].bitcast(I32), 0)
        nc.vector.memset(first_s_raw[:].bitcast(I32), 0)
        nc.vector.memset(boards[0][:, 0:C], 0.0)

        stage_scales(nc.gpsimd, 1, w0_scales)
        for t in range(1, PACK):
            nc.gpsimd.memset(boards[t][:, 0:C], 0.0)
        nc.gpsimd.memset(last_s[:].bitcast(I32), 0)
        slope = load_rows(nc.gpsimd, "slope", sg)
        offset = load_rows(nc.gpsimd, "offset", bg)
        second_weight = load_rows(nc.gpsimd, "second_weight", sb)

        idx = load_list("idx", offs)
        load_words(nc.scalar, xt_w, xt_words[0])
        load_plane([nc.scalar, nc.sync, nc.scalar, nc.sync], xt_s[:], xt_scales)
        stage_scales(nc.sync, 0, w_scales)
        load_words(nc.scalar, xo_w, xo_words[0].rearrange("p c t -> p (c t)"))
        load_plane([nc.sync] * QUADS, xo_s[:], xo_scales)
        load_words(nc.scalar, w_raw, w_words[0].rearrange("p c t -> p (c t)"))
        load_words(nc.scalar, w0_raw, w0_words[0])
        warm_in = sb_tile("warm_in", [P, 1], F32)
        warm_out = sb_tile("warm_out", [P, 1], F32)
        nc.vector.memset(warm_in[:], 0.0)
        nc.scalar.activation(warm_out[:], warm_in[:], ACT.Sigmoid)
        idx2 = load_list("idx2", offs2)
        first_weight = load_rows(nc.scalar, "first_weight", sa)
        idx3 = load_list("idx3", offs3)
        idx7 = load_list("idx7", offs7)
        idx5 = load_list("idx5", offs5)
        idx4 = load_list("idx4", offs4)
        ws_w = sb_tile("ws_w", [P, N], U32)
        wb_w = sb_tile("wb_w", [P, N], U16)
        load_words(nc.sync, ws_w, ws_words[0].rearrange("p c t -> p (c t)"))
        load_plane([nc.sync] * QUADS, last_s[:, 0:N], ws_scales)
        load_words(nc.sync, wb_w, wb_words[0])
        load_plane([nc.sync] * QUADS, last_s[:, N : 2 * N], wb_scales)
        idx6 = load_list("idx6", offs6)

        def gather(name, table, lst, dtype):
            picked = sb_tile(name, [P, 16 * lst.shape[1]], dtype)
            nc.vector.tensor_copy(picked[:], table[:].indirect(lst))
            return picked

        tok_w = gather("tok_w", xt_w, idx[:], U16)
        tok_s = gather("tok_s", xt_s, idx[:], U8)
        for q in range(QUADS):
            nc.vector.tensor_copy(first_s_raw[:].bitcast(I32)[32 * q : 32 * q + 4, :], first_s_stage[:, q, :])
        by_slot = first_s_raw[:].rearrange("p (s m t) -> p s t m", s=2, t=PACK)
        first_s_head = sb_tile("first_s_head", [P, 2, 1, P], U8)
        nc.vector.tensor_copy(first_s_head[:], by_slot[:, :, 0:1, :])

        note_w = sb_tile("note_w", [P, J], U32)
        note_s = sb_tile("note_s", [P, J], U8)
        for h in range(2):
            part = idx2[:, h * (P // 16) : (h + 1) * (P // 16)]
            nc.vector.tensor_copy(note_w[:, h * P : (h + 1) * P], xo_w[:].indirect(part))
            nc.vector.tensor_copy(note_s[:, h * P : (h + 1) * P], xo_s[:].indirect(part))

        w_head = sb_tile("w_head", [P, 1, P], U32)
        w0_head = sb_tile("w0_head", [P, 1, P], U16)
        w_rest = sb_tile("w_rest", [P, PACK - 1, P], U32)
        w_by_slot = w_raw[:].rearrange("p (m t) -> p t m", t=PACK)
        w0_by_slot = w0_raw[:].rearrange("p (m t) -> p t m", t=PACK)
        nc.scalar.copy(w_head[:], w_by_slot[:, 0:1, :])
        nc.scalar.copy(w0_head[:], w0_by_slot[:, 0:1, :])
        nc.scalar.copy(w_rest[:].rearrange("p t m -> p m t"), w_raw[:].rearrange("p (m t) -> p m t", t=PACK)[:, :, 1:PACK])
        first_s_rest = keep.tile([P, 2, PACK - 1, P], U8, name="first_s_rest", tag="xo_w", align_bytes=64)
        nc.vector.tensor_copy(first_s_rest[:], by_slot[:, :, 1:PACK, :])
        w0_rest = keep.tile([P, PACK - 1, P], U16, name="w0_rest", tag="xo_s", align_bytes=64)
        nc.vector.tensor_copy(w0_rest[:], w0_by_slot[:, 1:PACK, :])

        def first_stage(acc, w_cols, w0_cols, scales, u, cols):
            nc.tensor.matmul_mx(acc, lhsT=w_cols[:, u, :].bitcast(E4M3), lhsT_scale=scales[:, 0, u, :],
                                rhs=tok_w[:, cols].bitcast(E2M1), rhs_scale=tok_s[:, cols], start=True, stop=False)
            nc.tensor.matmul_mx(acc, lhsT=w0_cols[:, u, :].bitcast(E2M1), lhsT_scale=scales[:, 1, u, :],
                                rhs=note_w[:, cols].bitcast(E4M3), rhs_scale=note_s[:, cols], start=False, stop=True)

        for h in range(2):
            acc = psum.tile([P, P], F32, name="head_acc%d" % h)
            first_stage(acc[:], w_head, w0_head, first_s_head, 0, slice(h * P, (h + 1) * P))
            head = sb_tile("head%d" % h, [P, P], F32)
            if h == 0:
                nc.scalar.copy(head[:], acc[:])
            else:
                nc.vector.tensor_copy(head[:], acc[:])
            nc.scalar.activation(boards[0][:].indirect(idx3[:, h * (P // 16) : (h + 1) * (P // 16)]), head[:], ACT.Copy)

        acc1 = psum.tile([P, J], F32, name="acc1")
        first_stage(acc1[:], w_rest, w0_rest, first_s_rest, 0, slice(0, J))
        hidden1 = sb_tile("hidden1", [P, J], F32)
        nc.vector.tensor_copy(hidden1[:], acc1[:])
        nc.vector.tensor_copy(boards[1][:].indirect(idx3[:]), hidden1[:])
        acc23 = psum.tile([P, 2, J], F32, name="acc23")
        for u in range(2):
            first_stage(acc23[:, u, :], w_rest, w0_rest, first_s_rest, 1 + u, slice(0, J))
        hidden23 = sb_tile("hidden23", [P, 2, J], F32)
        nc.vector.tensor_copy(hidden23[:], acc23[:])
        for u in range(2):
            nc.vector.tensor_copy(boards[2 + u][:].indirect(idx3[:]), hidden23[:, u, :])

        short_w = keep.tile([P, O], U16, name="short_w", tag="w_head", align_bytes=64)
        nc.vector.tensor_copy(short_w[:], xt_w[:].indirect(idx7[:]))
        short_s = keep.tile([P, O], U8, name="short_s", tag="first_s_head", align_bytes=64)
        nc.vector.tensor_copy(short_s[:], xt_s[:].indirect(idx7[:]))

        result_acc = {}
        for h in range(2):
            for b in range(N // P):
                acc = psum.tile([P, HALF], F32, name="result_acc%d%d" % (h, b))
                nc.tensor.matmul_mx(acc[:], lhsT=ws_w[:, b * P : (b + 1) * P].bitcast(E4M3),
                                    lhsT_scale=last_s[:, b * P : (b + 1) * P],
                                    rhs=short_w[:, h * HALF : (h + 1) * HALF].bitcast(E2M1),
                                    rhs_scale=short_s[:, h * HALF : (h + 1) * HALF], start=True, stop=False)
                result_acc[(h, b)] = acc

        kept = []
        for t in range(PACK):
            gate = sb_tile("gate%d" % t, [P, C], F32)
            weighted = sb_tile("weighted%d" % t, [P, C], F32)
            gated = sb_tile("gated%d" % t, [P, C], F32)
            kept_t = sb_tile("kept%d" % t, [P, C], F32)
            parts = 2 if t == PACK - 1 else 1
            for part in range(parts):
                cols = slice(part * C // parts, (part + 1) * C // parts)
                entries = slice(cols.start // 16, cols.stop // 16)
                nc.scalar.activation(gate[:, cols], boards[t][:].indirect(idx5[:, entries]), ACT.Sigmoid,
                                     bias=offset[:, t : t + 1], scale=slope[:, t : t + 1])
                nc.scalar.activation(weighted[:, cols], boards[t][:].indirect(idx4[:, entries]), ACT.Copy,
                                     scale=first_weight[:, t : t + 1])
                nc.vector.tensor_tensor(gated[:, cols], weighted[:, cols], gate[:, cols], ALU.mult)
                nc.vector.tensor_tensor(kept_t[:, cols], boards[t][:, cols], gated[:, cols], ALU.max)
            kept.append(kept_t)

        out_view = out.rearrange("(b p) o -> p b o", p=P)
        for h in range(2):
            hid = sb_tile("hid%d" % h, [P, PACK, HALF], F32)
            cols = HALF // 16
            for t in range(PACK):
                nc.scalar.activation(hid[:, t, :], kept[t][:].indirect(idx6[:, h * cols : (h + 1) * cols]), ACT.Copy,
                                     scale=second_weight[:, t : t + 1])
            woven = sb_tile("woven%d" % h, [P, HALF, PACK], BF16)
            nc.vector.tensor_copy(woven[:].rearrange("p (c i) t -> p c t i", i=4),
                                  hid[:].rearrange("p t (c i) -> p c t i", i=4))
            hid_w = sb_tile("hid_w%d" % h, [P, HALF], U32)
            hid_s = sb_tile("hid_s%d" % h, [P, HALF], U8)
            nc.vector.quantize_mx(hid_w[:].bitcast(E5M2), hid_s[:], woven[:].rearrange("p c t -> p (c t)"))
            result = sb_tile("result%d" % h, [P, N // P, HALF], F32)
            for b in range(N // P):
                acc = result_acc[(h, b)]
                nc.tensor.matmul_mx(acc[:], lhsT=wb_w[:, b * P : (b + 1) * P].bitcast(E2M1),
                                    lhsT_scale=last_s[:, N + b * P : N + (b + 1) * P],
                                    rhs=hid_w[:].bitcast(E5M2), rhs_scale=hid_s[:], start=False, stop=True)
                if (h, b) == (1, 0):
                    nc.vector.tensor_copy(result[:, b, :], acc[:])
                else:
                    nc.scalar.copy(result[:, b, :], acc[:])
            if h == 0:
                nc.sync.dma_start(out_view[:, :, 0:HALF], result[:])
            else:
                nc.sync.dma_start(out_view[:, 0, HALF:O], result[:, 0, :])
                nc.scalar.dma_start(out_view[:, 1, HALF:O], result[:, 1, :])
